import numpy as np
import ml_dtypes


def mxq(x, axis, fmt="e4m3"):
    dtype, down = {"e4m3": (ml_dtypes.float8_e4m3fn, 7), "e5m2": (ml_dtypes.float8_e5m2, 14)}[fmt]
    v = np.moveaxis(np.asarray(x, np.float32).astype(ml_dtypes.bfloat16).astype(np.float64), axis, -1)
    blocks = v.reshape(v.shape[:-1] + (-1, 32))
    amax = np.abs(blocks).max(-1, keepdims=True)
    byte = np.maximum(np.where(amax > 0, np.frexp(amax)[1] - 1 + 127, 0) - down, 1)
    scale = np.exp2(byte - 127.0)
    codes = (blocks / scale).astype(np.float32).astype(dtype).astype(np.float64)
    return np.moveaxis((codes * scale).reshape(v.shape), -1, axis)


WIDE = False


def mx_kscale(k):
    if not WIDE:
        return np.ones(k)
    levels = np.array([10, -10, 5, -5, 0])
    if k % 512:
        return np.exp2(np.random.permutation(np.resize(levels, k // 32))).repeat(32)
    a = np.empty((k // 512, 16))
    for p in range(k // 512):
        a[p, :8] = np.random.permutation(np.resize(levels, 8))
        for g in range(8):
            far = levels[np.abs(levels - a[p, g]) >= 10]
            a[p, g + 8] = far[np.random.randint(len(far))]
    return np.exp2(a.ravel()).repeat(32)


def f64(x):
    return np.asarray(x).astype(np.float64)


def striped(idx):
    return np.tile(idx.reshape(-1, 16).T, (8, 1)).astype(np.uint16)


def unstriped(offs):
    return offs[:16].T.reshape(-1).astype(np.int64)


E2M1 = np.array([0.0, 0.5, 1.0, 1.5, 2.0, 3.0, 4.0, 6.0, -0.0, -0.5, -1.0, -1.5, -2.0, -3.0, -4.0, -6.0])


def pack_weight(w, fmt):
    k, n = w.shape
    w = f64(np.asarray(w, np.float32).astype(ml_dtypes.bfloat16)).reshape(k // 32, 32, n)
    amax = np.abs(w).max(1)
    if fmt == "e4m3":
        byte = np.frexp(amax)[1] - 1 + 127 - 7
    else:
        mant, ex = np.frexp(amax / 6.0)
        byte = np.where(mant > 0.5, ex, ex - 1) + 127
    byte = np.clip(np.where(amax > 0, byte, 1), 1, 254)
    scaled = (w * np.exp2(127.0 - byte)[:, None, :]).reshape(k, n).astype(np.float32)
    by_word = np.ascontiguousarray(scaled.reshape(k // 512, 128, 4, n).transpose(0, 1, 3, 2))
    if fmt == "e4m3":
        words = by_word.astype(ml_dtypes.float8_e4m3fn).view(np.uint8)
    else:
        c = by_word.astype(ml_dtypes.float4_e2m1fn).view(np.uint8) & 0xF
        words = (c[..., 0::2] | (c[..., 1::2] << 4)).reshape(k // 512, 128, 2 * n)
    return np.ascontiguousarray(words), np.ascontiguousarray(byte.astype(np.uint8).reshape(k // 512, 16, n))


def unpack_weight(words, scales, fmt):
    g, _, n = scales.shape
    words = np.ascontiguousarray(words).reshape(g, 128, n, -1)
    if fmt == "e4m3":
        vals = words.view(ml_dtypes.float8_e4m3fn).astype(np.float64)
    else:
        nib = np.empty((g, 128, n, 4), np.uint8)
        nib[..., 0::2] = words & 0xF
        nib[..., 1::2] = words >> 4
        vals = E2M1[nib]
    vals = vals * np.repeat(np.exp2(scales.astype(np.float64) - 127.0), 8, axis=1)[..., None]
    return vals.transpose(0, 1, 3, 2).reshape(g * 512, n)


def gelu(v):
    return 0.5 * v * (1.0 + np.tanh(np.sqrt(2.0 / np.pi) * (v + 0.044715 * v**3)))


K, KA, H, T, S, T2, P = 1536, 1024, 1024, 4096, 1024, 2048, 512


def setup_inputs():
    n = np.random.standard_normal
    s = mx_kscale(K)[:, None]
    u = mx_kscale(H)[:, None]
    tab_words, tab_scales = pack_weight(n((K, T)) * s, "e4m3")
    w4_words, w4_scales = pack_weight(n((KA, H)) / np.sqrt(K) / s[:KA] * u.T, "e2m1")
    return {
        "tab_words": tab_words, "tab_scales": tab_scales,
        "w4_words": w4_words, "w4_scales": w4_scales,
        "w1": (n((K - KA, H)) / np.sqrt(K) / s[KA:] * u.T).astype(np.float32),
        "por": np.exp(0.4 * n((H, S))).astype(np.float32),
        "wgs": np.exp(0.3 * n((128, S))).astype(np.float32),
        "page0": (n((H, T2)) * u).astype(np.float32),
        "flo1": ((0.5 * n(H) - 0.2) * u[:, 0]).astype(np.float32),
        "flo2": ((0.5 * n(H) - 0.2) * u[:, 0]).astype(np.float32),
        "gain": (1.6 * n(H) / np.sqrt(H) / u[:, 0] ** 2).astype(np.float32),
        "lot": (0.8 * n(P)).astype(np.float32),
        "duty": np.exp(0.5 * n(P)).astype(np.float32),
        "offs": striped(np.random.permutation(T)[:S]),
        "offs2": striped(np.random.permutation(T2)[:S]),
        "offs3": striped(np.random.permutation(T2)[:P]),
        "offs4": striped(np.random.permutation(T2)[:P]),
    }


def reference(tab_words, tab_scales, w4_words, w4_scales, w1, por, wgs, page0, flo1, flo2, gain, lot, duty, offs, offs2, offs3, offs4):
    v = unpack_weight(tab_words, tab_scales, "e4m3")[:, unstriped(offs)]
    w4 = unpack_weight(w4_words, w4_scales, "e2m1")
    w1q = mxq(f64(w1), 0, "e4m3")
    h = (w4.T @ v[:KA] + w1q.T @ v[KA:]) * f64(por)
    page = f64(page0).copy()
    page[:, unstriped(offs2)] = np.tile(f64(wgs), (H // 128, 1)) * h
    x1 = np.maximum(page[:, unstriped(offs3)], f64(flo1)[:, None])
    x2 = np.maximum(page[:, unstriped(offs4)], f64(flo2)[:, None]) * f64(gain)[:, None]
    e = mxq(x1, 0, "e4m3").T @ mxq(x2, 0, "e4m3")
    return np.tanh(e + f64(lot)[:, None]) * f64(duty)[None, :]

@@ -1,0 +1,257 @@
+from contextlib import ExitStack
+
+import concourse.mybir as mybir
+
+K, KA, H, T, S, T2, NP = 1536, 1024, 1024, 4096, 1024, 2048, 512
+FLOPS = 2 * K * H * S + 2 * H * NP * NP
+
+F32 = mybir.dt.float32
+BF16 = mybir.dt.bfloat16
+I32 = mybir.dt.int32
+U32 = mybir.dt.uint32
+U16 = mybir.dt.uint16
+U8 = mybir.dt.uint8
+FP8X4 = mybir.dt.float8_e4m3fn_x4
+FP4X4 = mybir.dt.float4_e2m1fn_x4
+ALU = mybir.AluOpType
+ACT = mybir.ActivationFunctionType
+
+P = 128
+BANK = 512
+BLOCKS = H // P
+
+
+def tile_list_sinter_lot_grading_kernel(
+    tc, tab_words, tab_scales, w4_words, w4_scales, w1, por, wgs, page0, flo1, flo2, gain, lot, duty,
+    offs, offs2, offs3, offs4, out,
+):
+    nc = tc.nc
+    with ExitStack() as ctx:
+        keep = ctx.enter_context(tc.tile_pool(name="keep", bufs=1))
+        ring = ctx.enter_context(tc.tile_pool(name="ring", bufs=3))
+        psum = ctx.enter_context(tc.psum_pool(name="psum", bufs=1))
+
+        list1 = keep.tile([P, S // 16], U16, name="list1")
+        list2 = keep.tile([P, S // 16], U16, name="list2")
+        list3 = keep.tile([P, NP // 16], U16, name="list3")
+        list4 = keep.tile([P, NP // 16], U16, name="list4")
+        nc.sync.dma_start(list1[:], offs)
+
+        tscale = keep.tile([P, T], U8, name="tscale", align_bytes=64)
+        w4s_raw = keep.tile([P, 2, H], U8, name="w4s_raw", align_bytes=64)
+        v_scale = keep.tile([P, S], U8, name="v_scale", align_bytes=64)
+        v_scale1 = keep.tile([P, S], U8, name="v_scale1", align_bytes=64)
+        nc.vector.memset(tscale[:].bitcast(I32), 0)
+        nc.vector.memset(w4s_raw[:].rearrange("p a n -> p (a n)").bitcast(I32), 0)
+        nc.vector.memset(v_scale1[:].bitcast(I32), 0)
+        for q in range(4):
+            nc.gpsimd.dma_start(
+                out=tscale[32 * q : 32 * q + 12, :].bitcast(I32),
+                in_=tab_scales[:, 4 * q : 4 * q + 4, :].bitcast(I32),
+            )
+        for q in range(4):
+            nc.gpsimd.dma_start(
+                out=w4s_raw[32 * q : 32 * q + 4, :, :].bitcast(I32),
+                in_=w4_scales[:, 4 * q : 4 * q + 4, :].rearrange("a r n -> r a n").bitcast(I32),
+            )
+
+        w4_raw = keep.tile([P, 2, 2 * H], U8, name="w4_raw", align_bytes=64)
+        nc.sync.dma_start(out=w4_raw[:].bitcast(I32), in_=w4_words.rearrange("a p n -> p a n").bitcast(I32))
+
+        table = [keep.tile([P, T], I32, name=f"table{a}", align_bytes=64) for a in range(3)]
+        v_words = [keep.tile([P, S], U32, name=f"v_words{a}", align_bytes=64) for a in range(3)]
+        w1_codes = keep.tile([P, H], U32, name="w1_codes", align_bytes=64)
+        w1_scale = keep.tile([P, H], U8, name="w1_scale", align_bytes=64)
+
+        def load_table(a):
+            nc.sync.dma_start(out=table[a][:], in_=tab_words[a].rearrange("p n t -> p (n t)").bitcast(I32))
+
+        def quantise_w1(b):
+            raw = ring.tile([P, 4, BANK], F32, name="w1_raw", bufs=1)
+            nc.sync.dma_start(out=raw[:], in_=w1[:, BANK * b : BANK * (b + 1)].rearrange("(p j) c -> p j c", j=4))
+            grouped = ring.tile([P, 4, P, 4], BF16, name="w1_grouped", bufs=1, align_bytes=64)
+            nc.scalar.copy(out=grouped[:], in_=raw[:].rearrange("p j (q t) -> p t q j", t=4))
+            cols = slice(BANK * b, BANK * (b + 1))
+            nc.vector.quantize_mx(
+                out=w1_codes[:, cols].bitcast(FP8X4),
+                scales=w1_scale[:, cols],
+                in_=grouped[:].rearrange("p t q j -> p (t q j)"),
+            )
+
+        load_table(0)
+        nc.vector.tensor_copy(v_scale[:], tscale[:].indirect(list1[:]))
+        nc.gpsimd.dma_start(out=v_scale1[0:112, :].bitcast(I32), in_=v_scale[4:116, :].bitcast(I32))
+
+        w4_codes = keep.tile([P, 2, 2 * H], U8, name="w4_codes", align_bytes=64)
+        w4_scale = keep.tile([P, 2, H], U8, name="w4_scale", align_bytes=64)
+        nc.vector.tensor_copy(
+            out=w4_codes[:].bitcast(U16).rearrange("p a (b t q) -> p (a b) t q", b=2, t=4),
+            in_=w4_raw[:].bitcast(U16).rearrange("p a (b q t) -> p (a b) t q", b=2, t=4),
+        )
+        nc.vector.tensor_copy(
+            out=w4_scale[:].rearrange("p a (b t q) -> p (a b) t q", b=2, t=4),
+            in_=w4s_raw[:].rearrange("p a (b q t) -> p (a b) t q", b=2, t=4),
+        )
+        nc.vector.tensor_copy(v_words[0][:], table[0][:].bitcast(U32).indirect(list1[:]))
+        quantise_w1(0)
+        load_table(1)
+        nc.vector.tensor_copy(v_words[1][:], table[1][:].bitcast(U32).indirect(list1[:]))
+        load_table(2)
+        for half in range(2):
+            nc.vector.tensor_copy(
+                v_words[2][:, BANK * half : BANK * (half + 1)],
+                table[2][:].bitcast(U32).indirect(list1[:, 32 * half : 32 * (half + 1)]),
+            )
+
+        wgs_dealt = [keep.tile([P, S], F32, name=f"wgs_dealt{t}") for t in range(4)]
+        floors1 = keep.tile([P, 2, 4], F32, name="floors1")
+        floors2 = keep.tile([P, 2, 4], F32, name="floors2")
+        gains = keep.tile([P, 2, 4], F32, name="gains")
+        lots = keep.tile([P, 4], F32, name="lots")
+        duties = keep.tile([P, NP], F32, name="duties")
+
+        planes = {}
+        grouped = {}
+        codes = {}
+        scales = {}
+        for b in range(2):
+            for x in range(2):
+                planes[b, x] = keep.tile([P, 4, NP], BF16, name=f"planes{b}{x}", align_bytes=64)
+                grouped[b, x] = keep.tile([P, NP, 4], BF16, name=f"grouped{b}{x}", align_bytes=64)
+                codes[b, x] = keep.tile([P, NP], U32, name=f"codes{b}{x}", align_bytes=64)
+                scales[b, x] = keep.tile([P, NP], U8, name=f"scales{b}{x}", align_bytes=64)
+
+        h = {}
+        page = {}
+        picked = {}
+
+        def make_h(i):
+            b, t = divmod(i, 4)
+            weight = ring.tile([P, S], F32, name="weight", bufs=3)
+            nc.sync.dma_start(out=weight[:], in_=por.rearrange("(b p t) j -> b t p j", b=2, t=4)[b, t])
+            if b == 0:
+                for q in (0, 2, 1, 3):
+                    nc.sync.dma_start(
+                        out=wgs_dealt[t][32 * q : 32 * q + 32, :], in_=wgs.rearrange("(p t) j -> t p j", t=4)[t]
+                    )
+            page[i] = ring.tile([P, T2], F32, name="page", bufs=3)
+            nc.sync.dma_start(out=page[i][:], in_=page0.rearrange("(b p t) n -> b t p n", b=2, t=4)[b, t])
+            if i == 0:
+                nc.sync.dma_start(list2[:], offs2)
+                nc.sync.dma_start(list3[:], offs3)
+                nc.sync.dma_start(list4[:], offs4)
+            h[i] = ring.tile([P, S], F32, name="h", bufs=4)
+            rows = slice(P * i, P * (i + 1))
+            for half in range(2):
+                cols = slice(BANK * half, BANK * (half + 1))
+                acc = psum.tile([P, BANK], F32, name="acc", bufs=4)
+                for a in range(2):
+                    nc.tensor.matmul_mx(
+                        out=acc[:],
+                        lhsT=w4_codes[:, a, 2 * P * i : 2 * P * (i + 1)].bitcast(FP4X4),
+                        lhsT_scale=w4_scale[:, a, rows],
+                        rhs=v_words[a][:, cols].bitcast(FP8X4),
+                        rhs_scale=(v_scale, v_scale1)[a][:, cols],
+                        start=(a == 0),
+                        stop=False,
+                    )
+                nc.tensor.matmul_mx(
+                    out=acc[:],
+                    lhsT=w1_codes[:, rows].bitcast(FP8X4),
+                    lhsT_scale=w1_scale[:, rows],
+                    rhs=v_words[2][:, cols].bitcast(FP8X4),
+                    rhs_scale=v_scale[8:P, cols],
+                    start=False,
+                    stop=True,
+                )
+                nc.scalar.copy(out=h[i][:, cols], in_=acc[:])
+            nc.gpsimd.tensor_tensor(weight[:], weight[:], wgs_dealt[t][:], ALU.mult)
+            for half in range(2):
+                cols = slice(BANK * half, BANK * (half + 1))
+                nc.gpsimd.tensor_tensor(h[i][:, cols], h[i][:, cols], weight[:, cols], ALU.mult)
+
+        def through_page(i):
+            if i == 0:
+                for half in range(2):
+                    nc.vector.tensor_copy(
+                        page[i][:].indirect(list2[:, 32 * half : 32 * (half + 1)]),
+                        h[i][:, BANK * half : BANK * (half + 1)],
+                    )
+            else:
+                nc.vector.tensor_copy(page[i][:].indirect(list2[:]), h[i][:])
+            for x, picks in ((1, list4), (0, list3)):
+                picked[i, x] = ring.tile([P, NP], F32, name=f"picked{x}", bufs=3)
+                nc.vector.tensor_copy(picked[i, x][:], page[i][:].indirect(picks[:]))
+
+        def floor(i, x, engine):
+            b, t = divmod(i, 4)
+            if x == 0:
+                engine.tensor_scalar(planes[b, 0][:, t, :], picked[i, 0][:], floors1[:, b, t : t + 1], 1.0, ALU.max, ALU.mult)
+            else:
+                engine.tensor_scalar(
+                    planes[b, 1][:, t, :], picked[i, 1][:], floors2[:, b, t : t + 1], gains[:, b, t : t + 1], ALU.max, ALU.mult
+                )
+
+        def weave_all(b, x):
+            nc.scalar.copy(
+                out=grouped[b, x][:].rearrange("p (c i) t -> p c t i", i=4),
+                in_=planes[b, x][:].rearrange("p t (c i) -> p c t i", i=4),
+            )
+
+        def weave_pair(b, x, u, copy):
+            copy(out=grouped[b, x][:, :, 2 * u : 2 * u + 2], in_=planes[b, x][:, 2 * u : 2 * u + 2, :].rearrange("p t c -> p c t"))
+
+        def quantise(b, x):
+            nc.vector.quantize_mx(
+                out=codes[b, x][:].bitcast(FP8X4), scales=scales[b, x][:], in_=grouped[b, x][:].rearrange("p c t -> p (c t)")
+            )
+
+        make_h(0)
+        for vec, dst in ((flo1, floors1), (flo2, floors2), (gain, gains)):
+            nc.sync.dma_start(out=dst[:], in_=vec.rearrange("(b p t) -> p b t", b=2, t=4))
+        make_h(1)
+        quantise_w1(1)
+        for i in range(BLOCKS):
+            through_page(i)
+            if i + 2 < BLOCKS:
+                make_h(i + 2)
+            if i == 3:
+                with nc.allow_non_contiguous_dma(reason="one value of lot a partition"):
+                    nc.sync.dma_start(out=lots[:], in_=lot.rearrange("(c p) -> p c", p=P))
+                nc.sync.dma_start(out=duties[:], in_=duty.partition_broadcast(P))
+            if i < BLOCKS - 1:
+                for x in (1, 0):
+                    floor(i, x, nc.vector)
+            if i == 3:
+                for x in (1, 0):
+                    weave_all(0, x)
+            if i == 5:
+                for x in (1, 0):
+                    weave_pair(1, x, 0, nc.scalar.copy)
+            if i == 6:
+                for x in (1, 0):
+                    quantise(0, x)
+        floor(BLOCKS - 1, 1, nc.vector)
+        weave_pair(1, 1, 1, nc.scalar.copy)
+        floor(BLOCKS - 1, 0, nc.vector)
+        weave_pair(1, 0, 1, nc.vector.tensor_copy)
+        quantise(1, 1)
+        quantise(1, 0)
+
+        for c in range(4):
+            e = psum.tile([P, NP], F32, name=f"e{c}")
+            m_cols = slice(P * c, P * (c + 1))
+            for b in range(2):
+                nc.tensor.matmul_mx(
+                    out=e[:],
+                    lhsT=codes[b, 0][:, m_cols].bitcast(FP8X4),
+                    lhsT_scale=scales[b, 0][:, m_cols],
+                    rhs=codes[b, 1][:].bitcast(FP8X4),
+                    rhs_scale=scales[b, 1][:],
+                    start=(b == 0),
+                    stop=(b == 1),
+                )
+            graded = keep.tile([P, NP], F32, name=f"graded{c}")
+            nc.scalar.activation(graded[:], e[:], ACT.Tanh, bias=lots[:, c : c + 1])
+            nc.vector.tensor_tensor(graded[:], graded[:], duties[:], ALU.mult)
+            nc.sync.dma_start(out=out[m_cols, :], in_=graded[:])

@@ -19,6 +19,7 @@ ACT = mybir.ActivationFunctionType
 P = 128
 BANK = 512
 BLOCKS = H // P
+NO_CEILING = float("inf")
 
 
 def tile_list_sinter_lot_grading_kernel(
@@ -29,6 +30,7 @@ def tile_list_sinter_lot_grading_kernel(
     with ExitStack() as ctx:
         keep = ctx.enter_context(tc.tile_pool(name="keep", bufs=1))
         ring = ctx.enter_context(tc.tile_pool(name="ring", bufs=3))
+        placed = ctx.enter_context(tc.tile_pool(name="placed", bufs=1))
         psum = ctx.enter_context(tc.psum_pool(name="psum", bufs=1))
 
         list1 = keep.tile([P, S // 16], U16, name="list1")
@@ -96,6 +98,7 @@ def tile_list_sinter_lot_grading_kernel(
         quantise_w1(0)
         load_table(1)
         nc.vector.tensor_copy(v_words[1][:], table[1][:].bitcast(U32).indirect(list1[:]))
+        nc.sync.dma_start(list2[:], offs2)
         load_table(2)
         for half in range(2):
             nc.vector.tensor_copy(
@@ -110,37 +113,39 @@ def tile_list_sinter_lot_grading_kernel(
         lots = keep.tile([P, 4], F32, name="lots")
         duties = keep.tile([P, NP], F32, name="duties")
 
-        planes = {}
         grouped = {}
         codes = {}
         scales = {}
         for b in range(2):
             for x in range(2):
-                planes[b, x] = keep.tile([P, 4, NP], BF16, name=f"planes{b}{x}", align_bytes=64)
                 grouped[b, x] = keep.tile([P, NP, 4], BF16, name=f"grouped{b}{x}", align_bytes=64)
-                codes[b, x] = keep.tile([P, NP], U32, name=f"codes{b}{x}", align_bytes=64)
+                if b == 0:
+                    codes[b, x] = placed.tile([P, NP], U32, name=f"codes{b}{x}", align_bytes=64, offset=4 * S * 3 + 4 * NP * x)
+                else:
+                    codes[b, x] = keep.tile([P, NP], U32, name=f"codes{b}{x}", align_bytes=64)
                 scales[b, x] = keep.tile([P, NP], U8, name=f"scales{b}{x}", align_bytes=64)
 
         h = {}
+        weights = {}
         page = {}
         picked = {}
 
         def make_h(i):
             b, t = divmod(i, 4)
-            weight = ring.tile([P, S], F32, name="weight", bufs=3)
+            weight = ring.tile([P, S], F32, name="weight", bufs=4)
+            weights[i] = weight
             nc.sync.dma_start(out=weight[:], in_=por.rearrange("(b p t) j -> b t p j", b=2, t=4)[b, t])
             if b == 0:
                 for q in (0, 2, 1, 3):
-                    nc.sync.dma_start(
+                    (nc.scalar if t == 0 else nc.sync).dma_start(
                         out=wgs_dealt[t][32 * q : 32 * q + 32, :], in_=wgs.rearrange("(p t) j -> t p j", t=4)[t]
                     )
-            page[i] = ring.tile([P, T2], F32, name="page", bufs=3)
+            page[i] = ring.tile([P, T2], F32, name="page", bufs=4)
             nc.sync.dma_start(out=page[i][:], in_=page0.rearrange("(b p t) n -> b t p n", b=2, t=4)[b, t])
             if i == 0:
-                nc.sync.dma_start(list2[:], offs2)
                 nc.sync.dma_start(list3[:], offs3)
                 nc.sync.dma_start(list4[:], offs4)
-            h[i] = ring.tile([P, S], F32, name="h", bufs=4)
+            h[i] = placed.tile([P, S], F32, name=f"h{i}", offset=4 * S * (i % 4))
             rows = slice(P * i, P * (i + 1))
             for half in range(2):
                 cols = slice(BANK * half, BANK * (half + 1))
@@ -164,11 +169,14 @@ def tile_list_sinter_lot_grading_kernel(
                     start=False,
                     stop=True,
                 )
-                nc.scalar.copy(out=h[i][:, cols], in_=acc[:])
-            nc.gpsimd.tensor_tensor(weight[:], weight[:], wgs_dealt[t][:], ALU.mult)
-            for half in range(2):
-                cols = slice(BANK * half, BANK * (half + 1))
-                nc.gpsimd.tensor_tensor(h[i][:, cols], h[i][:, cols], weight[:, cols], ALU.mult)
+                if i == 0 and half == 0:
+                    nc.vector.tensor_tensor(weight[:, cols], weight[:, cols], wgs_dealt[t][:, cols], ALU.mult)
+                    nc.vector.tensor_tensor(h[i][:, cols], acc[:], weight[:, cols], ALU.mult)
+                else:
+                    nc.scalar.copy(out=h[i][:, cols], in_=acc[:])
+            rest = slice(BANK if i == 0 else 0, S)
+            nc.gpsimd.tensor_tensor(weight[:, rest], weight[:, rest], wgs_dealt[t][:, rest], ALU.mult)
+            nc.gpsimd.tensor_tensor(h[i][:, rest], h[i][:, rest], weight[:, rest], ALU.mult)
 
         def through_page(i):
             if i == 0:
@@ -180,30 +188,28 @@ def tile_list_sinter_lot_grading_kernel(
             else:
                 nc.vector.tensor_copy(page[i][:].indirect(list2[:]), h[i][:])
             for x, picks in ((1, list4), (0, list3)):
-                picked[i, x] = ring.tile([P, NP], F32, name=f"picked{x}", bufs=3)
-                nc.vector.tensor_copy(picked[i, x][:], page[i][:].indirect(picks[:]))
+                picked[i, x] = ring.tile([P, NP], F32, name=f"picked{x}", bufs=2)
+                pieces = 2 if (i, x) == (BLOCKS - 1, 1) else 1
+                for k in range(pieces):
+                    n = NP // pieces
+                    nc.vector.tensor_copy(
+                        picked[i, x][:, n * k : n * (k + 1)], page[i][:].indirect(picks[:, n // 16 * k : n // 16 * (k + 1)])
+                    )
 
-        def floor(i, x, engine):
+        def floor_duties(i, spare, cols):
             b, t = divmod(i, 4)
-            if x == 0:
-                engine.tensor_scalar(planes[b, 0][:, t, :], picked[i, 0][:], floors1[:, b, t : t + 1], 1.0, ALU.max, ALU.mult)
-            else:
-                engine.tensor_scalar(
-                    planes[b, 1][:, t, :], picked[i, 1][:], floors2[:, b, t : t + 1], gains[:, b, t : t + 1], ALU.max, ALU.mult
-                )
+            nc.gpsimd.tensor_scalar(spare[:, cols], picked[i, 1][:, cols], NO_CEILING, floors2[:, b, t : t + 1], ALU.min, ALU.max)
+            nc.scalar.activation(grouped[b, 1][:, cols, t], spare[:, cols], ACT.Copy, scale=gains[:, b, t : t + 1])
 
-        def weave_all(b, x):
-            nc.scalar.copy(
-                out=grouped[b, x][:].rearrange("p (c i) t -> p c t i", i=4),
-                in_=planes[b, x][:].rearrange("p t (c i) -> p c t i", i=4),
-            )
+        def floor_lots(i, spare):
+            b, t = divmod(i, 4)
+            nc.gpsimd.tensor_scalar(spare, picked[i, 0][:], NO_CEILING, floors1[:, b, t : t + 1], ALU.min, ALU.max)
 
-        def weave_pair(b, x, u, copy):
-            copy(out=grouped[b, x][:, :, 2 * u : 2 * u + 2], in_=planes[b, x][:, 2 * u : 2 * u + 2, :].rearrange("p t c -> p c t"))
-
-        def quantise(b, x):
+        def quantise(b, x, cols):
             nc.vector.quantize_mx(
-                out=codes[b, x][:].bitcast(FP8X4), scales=scales[b, x][:], in_=grouped[b, x][:].rearrange("p c t -> p (c t)")
+                out=codes[b, x][:, cols].bitcast(FP8X4),
+                scales=scales[b, x][:, cols],
+                in_=grouped[b, x][:, cols, :].rearrange("p c t -> p (c t)"),
             )
 
         make_h(0)
@@ -220,23 +226,24 @@ def tile_list_sinter_lot_grading_kernel(
                     nc.sync.dma_start(out=lots[:], in_=lot.rearrange("(c p) -> p c", p=P))
                 nc.sync.dma_start(out=duties[:], in_=duty.partition_broadcast(P))
             if i < BLOCKS - 1:
-                for x in (1, 0):
-                    floor(i, x, nc.vector)
-            if i == 3:
-                for x in (1, 0):
-                    weave_all(0, x)
-            if i == 5:
-                for x in (1, 0):
-                    weave_pair(1, x, 0, nc.scalar.copy)
-            if i == 6:
-                for x in (1, 0):
-                    quantise(0, x)
-        floor(BLOCKS - 1, 1, nc.vector)
-        weave_pair(1, 1, 1, nc.scalar.copy)
-        floor(BLOCKS - 1, 0, nc.vector)
-        weave_pair(1, 0, 1, nc.vector.tensor_copy)
-        quantise(1, 1)
-        quantise(1, 0)
+                floor_duties(i, weights[i + 1], slice(0, NP))
+                rounded = weights[i + 1][:, NP:S].bitcast(BF16)
+                floor_lots(i, rounded[:, 0:NP])
+                if i < BLOCKS - 2:
+                    nc.scalar.copy(out=grouped[i // 4, 0][:, :, i % 4], in_=rounded[:, 0:NP])
+        last = BLOCKS - 1
+        for k in range(2):
+            floor_duties(last, h[last - 1], slice(NP // 2 * k, NP // 2 * (k + 1)))
+        quantise(0, 1, slice(0, NP))
+        nc.vector.tensor_scalar_max(rounded[:, NP:S], picked[last, 0][:], floors1[:, 1, 3:4])
+        quantise(0, 0, slice(0, NP))
+        quantise(1, 1, slice(0, NP))
+        pair = rounded.rearrange("p (t c) -> p c t", t=2)
+        for c in range(5):
+            if c < 4:
+                nc.vector.tensor_copy(out=grouped[1, 0][:, P * c : P * (c + 1), 2:4], in_=pair[:, P * c : P * (c + 1), :])
+            if c > 0:
+                quantise(1, 0, slice(P * (c - 1), P * c))
 
         for c in range(4):
             e = psum.tile([P, NP], F32, name=f"e{c}")
@@ -252,6 +259,9 @@ def tile_list_sinter_lot_grading_kernel(
                     stop=(b == 1),
                 )
             graded = keep.tile([P, NP], F32, name=f"graded{c}")
-            nc.scalar.activation(graded[:], e[:], ACT.Tanh, bias=lots[:, c : c + 1])
-            nc.vector.tensor_tensor(graded[:], graded[:], duties[:], ALU.mult)
-            nc.sync.dma_start(out=out[m_cols, :], in_=graded[:])
+            pieces = 2 if c == 3 else 1
+            for k in range(pieces):
+                cols = slice(NP // pieces * k, NP // pieces * (k + 1))
+                nc.scalar.activation(graded[:, cols], e[:, cols], ACT.Tanh, bias=lots[:, c : c + 1])
+                nc.vector.tensor_tensor(graded[:, cols], graded[:, cols], duties[:, cols], ALU.mult)
+                nc.sync.dma_start(out=out[m_cols, cols], in_=graded[:, cols])

from contextlib import ExitStack

import concourse.mybir as mybir

K, KA, H, T, S, T2, NP = 1536, 1024, 1024, 4096, 1024, 2048, 512
FLOPS = 2 * K * H * S + 2 * H * NP * NP

F32 = mybir.dt.float32
BF16 = mybir.dt.bfloat16
I32 = mybir.dt.int32
U32 = mybir.dt.uint32
U16 = mybir.dt.uint16
U8 = mybir.dt.uint8
FP8X4 = mybir.dt.float8_e4m3fn_x4
FP4X4 = mybir.dt.float4_e2m1fn_x4
ALU = mybir.AluOpType
ACT = mybir.ActivationFunctionType

P = 128
BANK = 512
BLOCKS = H // P
NO_CEILING = float("inf")


def tile_list_sinter_lot_grading_kernel(
    tc, tab_words, tab_scales, w4_words, w4_scales, w1, por, wgs, page0, flo1, flo2, gain, lot, duty,
    offs, offs2, offs3, offs4, out,
):
    nc = tc.nc
    with ExitStack() as ctx:
        keep = ctx.enter_context(tc.tile_pool(name="keep", bufs=1))
        ring = ctx.enter_context(tc.tile_pool(name="ring", bufs=3))
        placed = ctx.enter_context(tc.tile_pool(name="placed", bufs=1))
        psum = ctx.enter_context(tc.psum_pool(name="psum", bufs=1))

        list1 = keep.tile([P, S // 16], U16, name="list1")
        list2 = keep.tile([P, S // 16], U16, name="list2")
        list3 = keep.tile([P, NP // 16], U16, name="list3")
        list4 = keep.tile([P, NP // 16], U16, name="list4")
        nc.sync.dma_start(list1[:], offs)

        tscale = keep.tile([P, T], U8, name="tscale", align_bytes=64)
        w4s_raw = keep.tile([P, 2, H], U8, name="w4s_raw", align_bytes=64)
        v_scale = keep.tile([P, S], U8, name="v_scale", align_bytes=64)
        v_scale1 = keep.tile([P, S], U8, name="v_scale1", align_bytes=64)
        nc.vector.memset(tscale[:].bitcast(I32), 0)
        nc.vector.memset(w4s_raw[:].rearrange("p a n -> p (a n)").bitcast(I32), 0)
        nc.vector.memset(v_scale1[:].bitcast(I32), 0)
        for q in range(4):
            nc.gpsimd.dma_start(
                out=tscale[32 * q : 32 * q + 12, :].bitcast(I32),
                in_=tab_scales[:, 4 * q : 4 * q + 4, :].bitcast(I32),
            )
        for q in range(4):
            nc.gpsimd.dma_start(
                out=w4s_raw[32 * q : 32 * q + 4, :, :].bitcast(I32),
                in_=w4_scales[:, 4 * q : 4 * q + 4, :].rearrange("a r n -> r a n").bitcast(I32),
            )

        w4_raw = keep.tile([P, 2, 2 * H], U8, name="w4_raw", align_bytes=64)
        nc.sync.dma_start(out=w4_raw[:].bitcast(I32), in_=w4_words.rearrange("a p n -> p a n").bitcast(I32))

        table = [keep.tile([P, T], I32, name=f"table{a}", align_bytes=64) for a in range(3)]
        v_words = [keep.tile([P, S], U32, name=f"v_words{a}", align_bytes=64) for a in range(3)]
        w1_codes = keep.tile([P, H], U32, name="w1_codes", align_bytes=64)
        w1_scale = keep.tile([P, H], U8, name="w1_scale", align_bytes=64)

        def load_table(a):
            nc.sync.dma_start(out=table[a][:], in_=tab_words[a].rearrange("p n t -> p (n t)").bitcast(I32))

        def quantise_w1(b):
            raw = ring.tile([P, 4, BANK], F32, name="w1_raw", bufs=1)
            nc.sync.dma_start(out=raw[:], in_=w1[:, BANK * b : BANK * (b + 1)].rearrange("(p j) c -> p j c", j=4))
            grouped = ring.tile([P, 4, P, 4], BF16, name="w1_grouped", bufs=1, align_bytes=64)
            nc.scalar.copy(out=grouped[:], in_=raw[:].rearrange("p j (q t) -> p t q j", t=4))
            cols = slice(BANK * b, BANK * (b + 1))
            nc.vector.quantize_mx(
                out=w1_codes[:, cols].bitcast(FP8X4),
                scales=w1_scale[:, cols],
                in_=grouped[:].rearrange("p t q j -> p (t q j)"),
            )

        load_table(0)
        nc.vector.tensor_copy(v_scale[:], tscale[:].indirect(list1[:]))
        nc.gpsimd.dma_start(out=v_scale1[0:112, :].bitcast(I32), in_=v_scale[4:116, :].bitcast(I32))

        w4_codes = keep.tile([P, 2, 2 * H], U8, name="w4_codes", align_bytes=64)
        w4_scale = keep.tile([P, 2, H], U8, name="w4_scale", align_bytes=64)
        nc.vector.tensor_copy(
            out=w4_codes[:].bitcast(U16).rearrange("p a (b t q) -> p (a b) t q", b=2, t=4),
            in_=w4_raw[:].bitcast(U16).rearrange("p a (b q t) -> p (a b) t q", b=2, t=4),
        )
        nc.vector.tensor_copy(
            out=w4_scale[:].rearrange("p a (b t q) -> p (a b) t q", b=2, t=4),
            in_=w4s_raw[:].rearrange("p a (b q t) -> p (a b) t q", b=2, t=4),
        )
        nc.vector.tensor_copy(v_words[0][:], table[0][:].bitcast(U32).indirect(list1[:]))
        quantise_w1(0)
        load_table(1)
        nc.vector.tensor_copy(v_words[1][:], table[1][:].bitcast(U32).indirect(list1[:]))
        nc.sync.dma_start(list2[:], offs2)
        load_table(2)
        for half in range(2):
            nc.vector.tensor_copy(
                v_words[2][:, BANK * half : BANK * (half + 1)],
                table[2][:].bitcast(U32).indirect(list1[:, 32 * half : 32 * (half + 1)]),
            )

        wgs_dealt = [keep.tile([P, S], F32, name=f"wgs_dealt{t}") for t in range(4)]
        floors1 = keep.tile([P, 2, 4], F32, name="floors1")
        floors2 = keep.tile([P, 2, 4], F32, name="floors2")
        gains = keep.tile([P, 2, 4], F32, name="gains")
        lots = keep.tile([P, 4], F32, name="lots")
        duties = keep.tile([P, NP], F32, name="duties")

        grouped = {}
        codes = {}
        scales = {}
        for b in range(2):
            for x in range(2):
                grouped[b, x] = keep.tile([P, NP, 4], BF16, name=f"grouped{b}{x}", align_bytes=64)
                if b == 0:
                    codes[b, x] = placed.tile([P, NP], U32, name=f"codes{b}{x}", align_bytes=64, offset=4 * S * 3 + 4 * NP * x)
                else:
                    codes[b, x] = keep.tile([P, NP], U32, name=f"codes{b}{x}", align_bytes=64)
                scales[b, x] = keep.tile([P, NP], U8, name=f"scales{b}{x}", align_bytes=64)

        h = {}
        weights = {}
        page = {}
        picked = {}

        def make_h(i):
            b, t = divmod(i, 4)
            weight = ring.tile([P, S], F32, name="weight", bufs=4)
            weights[i] = weight
            nc.sync.dma_start(out=weight[:], in_=por.rearrange("(b p t) j -> b t p j", b=2, t=4)[b, t])
            if b == 0:
                for q in (0, 2, 1, 3):
                    (nc.scalar if t == 0 else nc.sync).dma_start(
                        out=wgs_dealt[t][32 * q : 32 * q + 32, :], in_=wgs.rearrange("(p t) j -> t p j", t=4)[t]
                    )
            page[i] = ring.tile([P, T2], F32, name="page", bufs=4)
            nc.sync.dma_start(out=page[i][:], in_=page0.rearrange("(b p t) n -> b t p n", b=2, t=4)[b, t])
            if i == 0:
                nc.sync.dma_start(list3[:], offs3)
                nc.sync.dma_start(list4[:], offs4)
            h[i] = placed.tile([P, S], F32, name=f"h{i}", offset=4 * S * (i % 4))
            rows = slice(P * i, P * (i + 1))
            for half in range(2):
                cols = slice(BANK * half, BANK * (half + 1))
                acc = psum.tile([P, BANK], F32, name="acc", bufs=4)
                for a in range(2):
                    nc.tensor.matmul_mx(
                        out=acc[:],
                        lhsT=w4_codes[:, a, 2 * P * i : 2 * P * (i + 1)].bitcast(FP4X4),
                        lhsT_scale=w4_scale[:, a, rows],
                        rhs=v_words[a][:, cols].bitcast(FP8X4),
                        rhs_scale=(v_scale, v_scale1)[a][:, cols],
                        start=(a == 0),
                        stop=False,
                    )
                nc.tensor.matmul_mx(
                    out=acc[:],
                    lhsT=w1_codes[:, rows].bitcast(FP8X4),
                    lhsT_scale=w1_scale[:, rows],
                    rhs=v_words[2][:, cols].bitcast(FP8X4),
                    rhs_scale=v_scale[8:P, cols],
                    start=False,
                    stop=True,
                )
                if i == 0 and half == 0:
                    nc.vector.tensor_tensor(weight[:, cols], weight[:, cols], wgs_dealt[t][:, cols], ALU.mult)
                    nc.vector.tensor_tensor(h[i][:, cols], acc[:], weight[:, cols], ALU.mult)
                else:
                    nc.scalar.copy(out=h[i][:, cols], in_=acc[:])
            rest = slice(BANK if i == 0 else 0, S)
            nc.gpsimd.tensor_tensor(weight[:, rest], weight[:, rest], wgs_dealt[t][:, rest], ALU.mult)
            nc.gpsimd.tensor_tensor(h[i][:, rest], h[i][:, rest], weight[:, rest], ALU.mult)

        def through_page(i):
            if i == 0:
                for half in range(2):
                    nc.vector.tensor_copy(
                        page[i][:].indirect(list2[:, 32 * half : 32 * (half + 1)]),
                        h[i][:, BANK * half : BANK * (half + 1)],
                    )
            else:
                nc.vector.tensor_copy(page[i][:].indirect(list2[:]), h[i][:])
            for x, picks in ((1, list4), (0, list3)):
                picked[i, x] = ring.tile([P, NP], F32, name=f"picked{x}", bufs=2)
                pieces = 2 if (i, x) == (BLOCKS - 1, 1) else 1
                for k in range(pieces):
                    n = NP // pieces
                    nc.vector.tensor_copy(
                        picked[i, x][:, n * k : n * (k + 1)], page[i][:].indirect(picks[:, n // 16 * k : n // 16 * (k + 1)])
                    )

        def floor_duties(i, spare, cols):
            b, t = divmod(i, 4)
            nc.gpsimd.tensor_scalar(spare[:, cols], picked[i, 1][:, cols], NO_CEILING, floors2[:, b, t : t + 1], ALU.min, ALU.max)
            nc.scalar.activation(grouped[b, 1][:, cols, t], spare[:, cols], ACT.Copy, scale=gains[:, b, t : t + 1])

        def floor_lots(i, spare):
            b, t = divmod(i, 4)
            nc.gpsimd.tensor_scalar(spare, picked[i, 0][:], NO_CEILING, floors1[:, b, t : t + 1], ALU.min, ALU.max)

        def quantise(b, x, cols):
            nc.vector.quantize_mx(
                out=codes[b, x][:, cols].bitcast(FP8X4),
                scales=scales[b, x][:, cols],
                in_=grouped[b, x][:, cols, :].rearrange("p c t -> p (c t)"),
            )

        make_h(0)
        for vec, dst in ((flo1, floors1), (flo2, floors2), (gain, gains)):
            nc.sync.dma_start(out=dst[:], in_=vec.rearrange("(b p t) -> p b t", b=2, t=4))
        make_h(1)
        quantise_w1(1)
        for i in range(BLOCKS):
            through_page(i)
            if i + 2 < BLOCKS:
                make_h(i + 2)
            if i == 3:
                with nc.allow_non_contiguous_dma(reason="one value of lot a partition"):
                    nc.sync.dma_start(out=lots[:], in_=lot.rearrange("(c p) -> p c", p=P))
                nc.sync.dma_start(out=duties[:], in_=duty.partition_broadcast(P))
            if i < BLOCKS - 1:
                floor_duties(i, weights[i + 1], slice(0, NP))
                rounded = weights[i + 1][:, NP:S].bitcast(BF16)
                floor_lots(i, rounded[:, 0:NP])
                if i < BLOCKS - 2:
                    nc.scalar.copy(out=grouped[i // 4, 0][:, :, i % 4], in_=rounded[:, 0:NP])
        last = BLOCKS - 1
        for k in range(2):
            floor_duties(last, h[last - 1], slice(NP // 2 * k, NP // 2 * (k + 1)))
        quantise(0, 1, slice(0, NP))
        nc.vector.tensor_scalar_max(rounded[:, NP:S], picked[last, 0][:], floors1[:, 1, 3:4])
        quantise(0, 0, slice(0, NP))
        quantise(1, 1, slice(0, NP))
        pair = rounded.rearrange("p (t c) -> p c t", t=2)
        for c in range(5):
            if c < 4:
                nc.vector.tensor_copy(out=grouped[1, 0][:, P * c : P * (c + 1), 2:4], in_=pair[:, P * c : P * (c + 1), :])
            if c > 0:
                quantise(1, 0, slice(P * (c - 1), P * c))

        for c in range(4):
            e = psum.tile([P, NP], F32, name=f"e{c}")
            m_cols = slice(P * c, P * (c + 1))
            for b in range(2):
                nc.tensor.matmul_mx(
                    out=e[:],
                    lhsT=codes[b, 0][:, m_cols].bitcast(FP8X4),
                    lhsT_scale=scales[b, 0][:, m_cols],
                    rhs=codes[b, 1][:].bitcast(FP8X4),
                    rhs_scale=scales[b, 1][:],
                    start=(b == 0),
                    stop=(b == 1),
                )
            graded = keep.tile([P, NP], F32, name=f"graded{c}")
            pieces = 2 if c == 3 else 1
            for k in range(pieces):
                cols = slice(NP // pieces * k, NP // pieces * (k + 1))
                nc.scalar.activation(graded[:, cols], e[:, cols], ACT.Tanh, bias=lots[:, c : c + 1])
                nc.vector.tensor_tensor(graded[:, cols], graded[:, cols], duties[:, cols], ALU.mult)
                nc.sync.dma_start(out=out[m_cols, cols], in_=graded[:, cols])
